import numpy as np
import ml_dtypes


def mxq(x, axis, fmt="e4m3"):
    dtype, down = {"e4m3": (ml_dtypes.float8_e4m3fn, 7), "e5m2": (ml_dtypes.float8_e5m2, 14)}[fmt]
    v = np.moveaxis(np.asarray(x, np.float32).astype(ml_dtypes.bfloat16).astype(np.float64), axis, -1)
    blocks = v.reshape(v.shape[:-1] + (-1, 32))
    amax = np.abs(blocks).max(-1, keepdims=True)
    byte = np.maximum(np.where(amax > 0, np.frexp(amax)[1] - 1 + 127, 0) - down, 1)
    scale = np.exp2(byte - 127.0)
    codes = (blocks / scale).astype(np.float32).astype(dtype).astype(np.float64)
    return np.moveaxis((codes * scale).reshape(v.shape), -1, axis)


WIDE = False


def mx_kscale(k):
    if not WIDE:
        return np.ones(k)
    levels = np.array([10, -10, 5, -5, 0])
    if k % 512:
        return np.exp2(np.random.permutation(np.resize(levels, k // 32))).repeat(32)
    a = np.empty((k // 512, 16))
    for p in range(k // 512):
        a[p, :8] = np.random.permutation(np.resize(levels, 8))
        for g in range(8):
            far = levels[np.abs(levels - a[p, g]) >= 10]
            a[p, g + 8] = far[np.random.randint(len(far))]
    return np.exp2(a.ravel()).repeat(32)


def f64(x):
    return np.asarray(x).astype(np.float64)


def striped(idx):
    return np.tile(idx.reshape(-1, 16).T, (8, 1)).astype(np.uint16)


def unstriped(offs):
    return offs[:16].T.reshape(-1).astype(np.int64)


def pack_weight(w):
    k, n = w.shape
    w = f64(np.asarray(w, np.float32).astype(ml_dtypes.bfloat16)).reshape(k // 32, 32, n)
    amax = np.abs(w).max(1)
    byte = np.clip(np.where(amax > 0, np.frexp(amax)[1] - 1 + 127 - 7, 1), 1, 254)
    scaled = (w * np.exp2(127.0 - byte)[:, None, :]).reshape(k, n).astype(np.float32)
    words = np.ascontiguousarray(scaled.reshape(k // 512, 128, 4, n).transpose(0, 1, 3, 2)).astype(ml_dtypes.float8_e4m3fn).view(np.uint8)
    return words, np.ascontiguousarray(byte.astype(np.uint8).reshape(k // 512, 16, n))


def unpack_weight(words, scales):
    g, p, n, _ = words.shape
    vals = np.ascontiguousarray(words).view(ml_dtypes.float8_e4m3fn).astype(np.float64) * np.repeat(np.exp2(scales.astype(np.float64) - 127.0), 8, axis=1)[..., None]
    return vals.transpose(0, 1, 3, 2).reshape(g * 512, n)


E2M1 = np.array([0.0, 0.5, 1.0, 1.5, 2.0, 3.0, 4.0, 6.0, -0.0, -0.5, -1.0, -1.5, -2.0, -3.0, -4.0, -6.0])


def pack_fp4(w):
    k, n = w.shape
    w = f64(np.asarray(w, np.float32).astype(ml_dtypes.bfloat16)).reshape(k // 32, 32, n)
    amax = np.abs(w).max(1)
    mant, ex = np.frexp(amax / 6.0)
    byte = np.clip(np.where(amax > 0, np.where(mant > 0.5, ex, ex - 1) + 127, 1), 1, 254)
    scaled = (w * np.exp2(127.0 - byte)[:, None, :]).reshape(k, n).astype(np.float32)
    c = np.ascontiguousarray(scaled.reshape(k // 512, 128, 4, n).transpose(0, 1, 3, 2)).astype(ml_dtypes.float4_e2m1fn).view(np.uint8) & 0xF
    words = (c[..., 0::2] | (c[..., 1::2] << 4)).reshape(k // 512, 128, 2 * n)
    return np.ascontiguousarray(words), np.ascontiguousarray(byte.astype(np.uint8).reshape(k // 512, 16, n))


def unpack_fp4(words, scales):
    g, _, n = scales.shape
    words = np.ascontiguousarray(words).reshape(g, 128, n, 2)
    nib = np.empty((g, 128, n, 4), np.uint8)
    nib[..., 0::2] = words & 0xF
    nib[..., 1::2] = words >> 4
    vals = E2M1[nib] * np.repeat(np.exp2(scales.astype(np.float64) - 127.0), 8, axis=1)[..., None]
    return vals.transpose(0, 1, 3, 2).reshape(g * 512, n)


K, T, S, D, N, H = 1024, 2048, 512, 2, 256, 512


def setup_inputs():
    n = np.random.standard_normal
    s = mx_kscale(K)[:, None]
    u = mx_kscale(H)
    packed_xT = pack_weight(n((K, T)) * s)
    packed_w1 = pack_fp4(n((K, H)) / np.sqrt(K) / s)
    packed_w2 = pack_fp4(n((K, H)) / np.sqrt(K) / s)
    packed_w3 = pack_fp4(n((H, N)) / np.sqrt(H) / u[:, None])
    return {
        "x_words": packed_xT[0],
        "x_scales": packed_xT[1],
        "w1_words": packed_w1[0],
        "w1_scales": packed_w1[1],
        "w2_words": packed_w2[0],
        "w2_scales": packed_w2[1],
        "unit": (np.random.uniform(0.6, 1.4, (H, 1)) * u[:, None]).astype(np.float32),
        "w3_words": packed_w3[0],
        "w3_scales": packed_w3[1],
        "offs": striped(np.random.permutation(T)[:S]),
        "riv": striped(np.random.permutation(S)),
    }


def reference(x_words, x_scales, w1_words, w1_scales, w2_words, w2_scales, unit, w3_words, w3_scales, offs, riv):
    xq = unpack_weight(x_words, x_scales)[:, unstriped(offs)]
    hk = unpack_fp4(w2_words, w2_scales).T @ xq
    aff = np.log(np.exp(hk) + 1.0) + 0.2
    pr = unpack_fp4(w1_words, w1_scales).T @ xq
    press = np.log(np.exp(pr) + 1.0)
    kp = np.sqrt(aff * press + 0.02)
    kr = kp[:, unstriped(riv)]
    load = kp / (kp + kr + 1.0)
    mix = load.reshape(len(load), -1, D).sum(axis=2)
    sel = load / (np.repeat(mix, D, axis=1) + 0.2)
    flux = sel * press
    tr = load[:, unstriped(riv)]
    hid = f64(unit) * (flux - (0.5 * tr))
    return unpack_fp4(w3_words, w3_scales).T @ mxq(hid, 0, "e4m3")

@@ -1,0 +1,218 @@
+from contextlib import ExitStack
+
+import concourse.mybir as mybir
+
+K, T, S, H, N = 1024, 2048, 512, 512, 256
+FLOPS = 2 * (2 * K * H * S + H * N * S)
+
+F32 = mybir.dt.float32
+BF16 = mybir.dt.bfloat16
+I32 = mybir.dt.int32
+U32 = mybir.dt.uint32
+U16 = mybir.dt.uint16
+U8 = mybir.dt.uint8
+FP8X4 = mybir.dt.float8_e4m3fn_x4
+FP4X4 = mybir.dt.float4_e2m1fn_x4
+ALU = mybir.AluOpType
+ACT = mybir.ActivationFunctionType
+
+P = 128
+PACK = 4
+PASSES = K // (P * PACK)
+QUADS = 4
+HALVES = 2
+HALF = S // HALVES
+EXP_CAP = 2.0 ** 56
+
+
+def tile_picked_yadsiso_flux_p_kernel(
+    tc, x_words, x_scales, w1_words, w1_scales, w2_words, w2_scales, unit, w3_words, w3_scales, offs, riv, out
+):
+    nc = tc.nc
+    with ExitStack() as ctx:
+        lists = ctx.enter_context(tc.tile_pool(name="lists", bufs=1))
+        keep = ctx.enter_context(tc.tile_pool(name="keep", bufs=1))
+        work = ctx.enter_context(tc.tile_pool(name="work", bufs=1))
+        psum = ctx.enter_context(tc.psum_pool(name="psum", bufs=1))
+
+        def load_scale_rows(queue, tile, scales):
+            for q in range(QUADS):
+                queue.dma_start(
+                    tile[32 * q : 32 * q + 4, :, :].bitcast(I32),
+                    scales[:, 4 * q : 4 * q + 4, :].rearrange("o r c -> r o c").bitcast(I32),
+                )
+
+        offs_sb = lists.tile([P, S // 16], U16, name="offs_sb")
+        riv_sb = lists.tile([P, S // 16], U16, name="riv_sb")
+        nc.sync.dma_start(offs_sb[:], offs)
+        nc.sync.dma_start(riv_sb[:], riv)
+
+        x_bytes = keep.tile([P, PASSES, T], U8, name="x_bytes", align_bytes=64)
+        nc.vector.memset(x_bytes[:].bitcast(I32), 0)
+        load_scale_rows(nc.scalar, x_bytes, x_scales)
+
+        raw_bytes = {}
+        for name, scales in (("w2", w2_scales), ("w1", w1_scales)):
+            raw_bytes[name] = keep.tile([P, PASSES, H], U8, name=name + "_raw_bytes", align_bytes=64)
+            (nc.gpsimd if name == "w2" else nc.vector).memset(raw_bytes[name][:].bitcast(I32), 0)
+            load_scale_rows(nc.gpsimd if name == "w2" else nc.sync, raw_bytes[name], scales)
+
+        x_table = [keep.tile([P, T], I32, name="x_table%d" % o, align_bytes=64) for o in range(PASSES)]
+        raw_words = {}
+        nc.sync.dma_start(x_table[0][:], x_words[0].rearrange("p n t -> p (n t)").bitcast(I32))
+        raw_words["w2"] = keep.tile([P, PASSES, 2 * H], U8, name="w2_raw_words", align_bytes=64)
+        nc.sync.dma_start(raw_words["w2"][:].bitcast(I32), w2_words.rearrange("o p c -> p o c").bitcast(I32))
+        nc.sync.dma_start(x_table[1][:], x_words[1].rearrange("p n t -> p (n t)").bitcast(I32))
+        raw_words["w1"] = keep.tile([P, PASSES, 2 * H], U8, name="w1_raw_words", align_bytes=64)
+        nc.sync.dma_start(raw_words["w1"][:].bitcast(I32), w1_words.rearrange("o p c -> p o c").bitcast(I32))
+
+        picked_words = [keep.tile([P, S], U32, name="picked_words%d" % o, align_bytes=64) for o in range(PASSES)]
+        picked_bytes = [keep.tile([P, S], U8, name="picked_bytes%d" % o, align_bytes=64) for o in range(PASSES)]
+        codes = {}
+        planes = {}
+
+        def deal(name, o):
+            codes[name, o] = keep.tile([P, 2 * H], U8, name="%s_codes%d" % (name, o), align_bytes=64)
+            planes[name, o] = keep.tile([P, H], U8, name="%s_bytes%d" % (name, o), align_bytes=64)
+            nc.vector.tensor_copy(
+                planes[name, o][:].rearrange("p (t m) -> p t m", t=PACK),
+                raw_bytes[name][:, o, :].rearrange("p (m t) -> p t m", t=PACK),
+            )
+            nc.vector.tensor_copy(
+                codes[name, o][:].rearrange("p (t m b) -> p t m b", t=PACK, b=2),
+                raw_words[name][:, o, :].rearrange("p (m t b) -> p t m b", t=PACK, b=2),
+            )
+
+        for o in range(PASSES):
+            nc.vector.tensor_copy(picked_bytes[o][:], x_bytes[:, o, :].indirect(offs_sb[:]))
+        nc.vector.tensor_copy(picked_words[0][:], x_table[0][:].bitcast(U32).indirect(offs_sb[:]))
+        deal("w2", 0)
+        deal("w2", 1)
+        nc.vector.tensor_copy(picked_words[1][:], x_table[1][:].bitcast(U32).indirect(offs_sb[:]))
+        deal("w1", 0)
+        deal("w1", 1)
+
+        unit_sb = keep.tile([P, PACK], F32, name="unit_sb", tag="w1_raw_words", align_bytes=64)
+        nc.sync.dma_start(unit_sb[:], unit.rearrange("(p t) o -> p (t o)", t=PACK))
+        w3_codes = keep.tile([P, 2 * N], U8, name="w3_codes", tag="w2_raw_words", align_bytes=64)
+        nc.sync.dma_start(w3_codes[:].bitcast(I32), w3_words[0].bitcast(I32))
+        w3_bytes = raw_bytes["w2"][:, 0:1, 0:N]
+        load_scale_rows(nc.sync, w3_bytes, w3_scales)
+
+        bank = {}
+        order = [("w2", t) for t in range(PACK)] + [("w1", t) for t in reversed(range(PACK))]
+        for name, t in order:
+            bank[name, t] = psum.tile([P, S], F32, name="bank_%s_%d" % (name, t))
+
+        def product(name, t, o):
+            nc.tensor.matmul_mx(
+                out=bank[name, t][:],
+                lhsT=codes[name, o][:, 2 * P * t : 2 * P * (t + 1)].bitcast(FP4X4),
+                lhsT_scale=planes[name, o][:, P * t : P * (t + 1)],
+                rhs=picked_words[o][:].bitcast(FP8X4),
+                rhs_scale=picked_bytes[o][:],
+                start=(o == 0),
+                stop=(o == PASSES - 1),
+            )
+
+        for name in ("w2", "w1"):
+            for o in range(PASSES):
+                for nm, t in order:
+                    if nm == name:
+                        product(name, t, o)
+
+        side = {"w2": 0, "w1": 1}
+        exps = [work.tile([P, 2, S], F32, name="exps%d" % t, tag="chain%d" % t) for t in range(PACK)]
+        for name, t in order:
+            nc.scalar.activation(exps[t][:, side[name], :], bank[name, t][:], ACT.Exp)
+            nc.vector.tensor_scalar(exps[t][:, side[name], :], exps[t][:, side[name], :], EXP_CAP, None, ALU.min)
+
+        aff = work.tile([P, PACK, S], F32, name="aff")
+        press = work.tile([P, PACK, S], F32, name="press")
+        prod = work.tile([P, PACK, S], F32, name="prod")
+        for t in range(PACK):
+            logs = work.tile([P, 2, S], F32, name="logs%d" % t, tag="chain%d" % (t - 1) if t else "logs")
+            nc.scalar.activation(logs[:], exps[t][:], ACT.Ln, bias=1.0)
+            nc.vector.tensor_tensor(aff[:, t, :], logs[:, 0, :], bank["w2", t][:], ALU.max)
+            nc.vector.tensor_tensor(press[:, t, :], logs[:, 1, :], bank["w1", t][:], ALU.max)
+            nc.vector.scalar_tensor_tensor(prod[:, t, :], aff[:, t, :], 0.2, press[:, t, :], ALU.add, ALU.mult)
+
+        halves = [(h, slice(h * HALF, (h + 1) * HALF), slice(h * HALF // 16, (h + 1) * HALF // 16)) for h in range(HALVES)]
+        VS = S // 2
+        cross = work.tile([P, PACK, S], F32, name="cross")
+        cross_press = work.tile([P, PACK, S], F32, name="cross_press")
+
+        all_dens = []
+
+        def by_pair(ap):
+            return ap.rearrange("p (v d) -> p v d", d=2)
+
+        for t in range(PACK):
+            kp = work.tile([P, S], F32, name="kp%d" % t)
+            nc.scalar.activation(kp[:], prod[:, t, :], ACT.Sqrt, bias=0.02)
+            rival = work.tile([P, S], F32, name="rival%d" % t)
+            for h, cols, entries in halves:
+                nc.scalar.activation(rival[:, cols], kp[:].indirect(riv_sb[:, entries]), ACT.Copy)
+            den = work.tile([P, S], F32, name="den%d" % t)
+            nc.vector.scalar_tensor_tensor(den[:], rival[:], 1.0, kp[:], ALU.add, ALU.add)
+            dens = work.tile([P, 2, VS], F32, name="dens%d" % t, tag="dens%d" % t)
+            nc.vector.tensor_tensor(by_pair(cross[:, t, :]), by_pair(kp[:]), by_pair(den[:])[:, :, ::-1], ALU.mult)
+            nc.vector.scalar_tensor_tensor(
+                dens[:, 0, :], by_pair(den[:])[:, :, 0], 2.0, by_pair(den[:])[:, :, 1], ALU.mult, ALU.mult
+            )
+            pair_sum = work.tile([P, VS], F32, name="pair_sum%d" % t)
+            nc.vector.tensor_tensor(pair_sum[:], by_pair(cross[:, t, :])[:, :, 0], by_pair(cross[:, t, :])[:, :, 1], ALU.add)
+            nc.vector.scalar_tensor_tensor(dens[:, 1, :], dens[:, 0, :], 0.1, pair_sum[:], ALU.mult, ALU.add)
+            all_dens.append(dens)
+        log_den = work.tile([P, PACK, S], F32, name="log_den", tag="prod")
+        for t in range(PACK):
+            nc.scalar.activation(log_den[:, t, :], all_dens[t][:].rearrange("p a v -> p (a v)"), ACT.Ln)
+        for t in range(PACK):
+            nc.vector.tensor_tensor(cross_press[:, t, :], cross[:, t, :], press[:, t, :], ALU.mult)
+
+        inv_den = work.tile([P, PACK, S], F32, name="inv_den", tag="dens%d" % (PACK - 1))
+        flux = work.tile([P, PACK, S], F32, name="flux")
+        loading = []
+        for t in range(PACK):
+            nc.scalar.activation(inv_den[:, t, :], log_den[:, t, :], ACT.Exp, scale=-1.0)
+            load_t = work.tile([P, S], F32, name="load%d" % t)
+            nc.vector.scalar_tensor_tensor(
+                by_pair(load_t[:]), by_pair(cross[:, t, :]), unit_sb[:, t : t + 1],
+                inv_den[:, t, 0:VS].unsqueeze(2).to_broadcast([P, VS, 2]), ALU.mult, ALU.mult,
+            )
+            loading.append(load_t)
+            nc.vector.scalar_tensor_tensor(
+                by_pair(flux[:, t, :]), by_pair(cross_press[:, t, :]), unit_sb[:, t : t + 1],
+                inv_den[:, t, VS:S].unsqueeze(2).to_broadcast([P, VS, 2]), ALU.mult, ALU.mult,
+            )
+
+        for h, cols, entries in halves:
+            rival_load = work.tile([P, PACK, HALF], F32, name="rival_load%d" % h)
+            for t in range(PACK):
+                nc.scalar.activation(rival_load[:, t, :], loading[t][:].indirect(riv_sb[:, entries]), ACT.Copy)
+            woven = work.tile([P, HALF, PACK], BF16, name="woven%d" % h, align_bytes=64)
+            nc.vector.tensor_tensor(
+                woven[:].rearrange("p (c i) t -> p c t i", i=4),
+                flux[:, :, cols].rearrange("p t (c i) -> p c t i", i=4),
+                rival_load[:].rearrange("p t (c i) -> p c t i", i=4),
+                ALU.subtract,
+            )
+            hid_codes = work.tile([P, HALF], U32, name="hid_codes%d" % h, align_bytes=64)
+            hid_bytes = work.tile([P, HALF], U8, name="hid_bytes%d" % h, align_bytes=64)
+            nc.vector.quantize_mx(
+                out=hid_codes[:].bitcast(FP8X4), scales=hid_bytes[:], in_=woven[:].rearrange("p c t -> p (c t)")
+            )
+            beds = psum.tile([P, N // P, HALF], F32, name="beds%d" % h, tag="bank_w2_%d" % h)
+            for c in range(N // P):
+                nc.tensor.matmul_mx(
+                    out=beds[:, c, :],
+                    lhsT=w3_codes[:, 2 * P * c : 2 * P * (c + 1)].bitcast(FP4X4),
+                    lhsT_scale=w3_bytes[:, 0, P * c : P * (c + 1)],
+                    rhs=hid_codes[:].bitcast(FP8X4),
+                    rhs_scale=hid_bytes[:],
+                    start=True,
+                    stop=True,
+                )
+            result = work.tile([P, N // P, HALF], F32, name="result%d" % h)
+            nc.scalar.copy(result[:], beds[:])
+            nc.sync.dma_start(out[:, cols].rearrange("(c p) j -> p c j", p=P), result[:])

@@ -22,6 +22,8 @@ PASSES = K // (P * PACK)
 QUADS = 4
 HALVES = 2
 HALF = S // HALVES
+CHUNKS = [(0, 256), (256, 128), (384, 128)]
+HOLD = ["rival_load0", "dens3", "cross"]
 EXP_CAP = 2.0 ** 56
 
 
@@ -35,8 +37,8 @@ def tile_picked_yadsiso_flux_p_kernel(
         work = ctx.enter_context(tc.tile_pool(name="work", bufs=1))
         psum = ctx.enter_context(tc.psum_pool(name="psum", bufs=1))
 
-        def load_scale_rows(queue, tile, scales):
-            for q in range(QUADS):
+        def load_scale_rows(queue, tile, scales, quads):
+            for q in quads:
                 queue.dma_start(
                     tile[32 * q : 32 * q + 4, :, :].bitcast(I32),
                     scales[:, 4 * q : 4 * q + 4, :].rearrange("o r c -> r o c").bitcast(I32),
@@ -44,63 +46,74 @@ def tile_picked_yadsiso_flux_p_kernel(
 
         offs_sb = lists.tile([P, S // 16], U16, name="offs_sb")
         riv_sb = lists.tile([P, S // 16], U16, name="riv_sb")
-        nc.sync.dma_start(offs_sb[:], offs)
-        nc.sync.dma_start(riv_sb[:], riv)
-
         x_bytes = keep.tile([P, PASSES, T], U8, name="x_bytes", align_bytes=64)
-        nc.vector.memset(x_bytes[:].bitcast(I32), 0)
-        load_scale_rows(nc.scalar, x_bytes, x_scales)
-
-        raw_bytes = {}
-        for name, scales in (("w2", w2_scales), ("w1", w1_scales)):
-            raw_bytes[name] = keep.tile([P, PASSES, H], U8, name=name + "_raw_bytes", align_bytes=64)
-            (nc.gpsimd if name == "w2" else nc.vector).memset(raw_bytes[name][:].bitcast(I32), 0)
-            load_scale_rows(nc.gpsimd if name == "w2" else nc.sync, raw_bytes[name], scales)
-
         x_table = [keep.tile([P, T], I32, name="x_table%d" % o, align_bytes=64) for o in range(PASSES)]
+        raw_bytes = {}
         raw_words = {}
-        nc.sync.dma_start(x_table[0][:], x_words[0].rearrange("p n t -> p (n t)").bitcast(I32))
-        raw_words["w2"] = keep.tile([P, PASSES, 2 * H], U8, name="w2_raw_words", align_bytes=64)
-        nc.sync.dma_start(raw_words["w2"][:].bitcast(I32), w2_words.rearrange("o p c -> p o c").bitcast(I32))
-        nc.sync.dma_start(x_table[1][:], x_words[1].rearrange("p n t -> p (n t)").bitcast(I32))
-        raw_words["w1"] = keep.tile([P, PASSES, 2 * H], U8, name="w1_raw_words", align_bytes=64)
-        nc.sync.dma_start(raw_words["w1"][:].bitcast(I32), w1_words.rearrange("o p c -> p o c").bitcast(I32))
+        for name in ("w2", "w1"):
+            raw_bytes[name] = keep.tile([P, PASSES, H], U8, name=name + "_raw_bytes", align_bytes=64)
+            raw_words[name] = keep.tile([P, PASSES, 2 * H], U8, name=name + "_raw_words", align_bytes=64)
+        nc.vector.memset(x_bytes[:, 0, :].bitcast(I32), 0)
+        nc.gpsimd.memset(x_bytes[:, 1, :].bitcast(I32), 0)
+        nc.vector.memset(raw_bytes["w2"][:].bitcast(I32), 0)
+        nc.vector.memset(raw_bytes["w1"][:].bitcast(I32), 0)
+
+        def load_table(o):
+            nc.sync.dma_start(x_table[o][:], x_words[o].rearrange("p n t -> p (n t)").bitcast(I32))
+
+        def load_words(name, words):
+            nc.sync.dma_start(raw_words[name][:].bitcast(I32), words.rearrange("o p c -> p o c").bitcast(I32))
+
+        nc.sync.dma_start(offs_sb[:], offs)
+        load_words("w2", w2_words)
+        load_scale_rows(nc.sync, x_bytes, x_scales, range(QUADS))
+        load_table(0)
+        load_scale_rows(nc.sync, raw_bytes["w2"], w2_scales, range(QUADS))
+        load_table(1)
+        load_words("w1", w1_words)
+        load_scale_rows(nc.sync, raw_bytes["w1"], w1_scales, range(QUADS))
+        nc.sync.dma_start(riv_sb[:], riv)
 
         picked_words = [keep.tile([P, S], U32, name="picked_words%d" % o, align_bytes=64) for o in range(PASSES)]
         picked_bytes = [keep.tile([P, S], U8, name="picked_bytes%d" % o, align_bytes=64) for o in range(PASSES)]
         codes = {}
         planes = {}
 
-        def deal(name, o):
+        def deal_words(name, o):
             codes[name, o] = keep.tile([P, 2 * H], U8, name="%s_codes%d" % (name, o), align_bytes=64)
-            planes[name, o] = keep.tile([P, H], U8, name="%s_bytes%d" % (name, o), align_bytes=64)
-            nc.vector.tensor_copy(
-                planes[name, o][:].rearrange("p (t m) -> p t m", t=PACK),
-                raw_bytes[name][:, o, :].rearrange("p (m t) -> p t m", t=PACK),
-            )
             nc.vector.tensor_copy(
                 codes[name, o][:].rearrange("p (t m b) -> p t m b", t=PACK, b=2),
                 raw_words[name][:, o, :].rearrange("p (m t b) -> p t m b", t=PACK, b=2),
             )
 
+        def deal_bytes(name, o):
+            planes[name, o] = keep.tile([P, H], U8, name="%s_bytes%d" % (name, o), align_bytes=64)
+            nc.vector.tensor_copy(
+                planes[name, o][:].rearrange("p (t m) -> p t m", t=PACK),
+                raw_bytes[name][:, o, :].rearrange("p (m t) -> p t m", t=PACK),
+            )
+
+        for o in range(PASSES):
+            deal_words("w2", o)
         for o in range(PASSES):
             nc.vector.tensor_copy(picked_bytes[o][:], x_bytes[:, o, :].indirect(offs_sb[:]))
         nc.vector.tensor_copy(picked_words[0][:], x_table[0][:].bitcast(U32).indirect(offs_sb[:]))
-        deal("w2", 0)
-        deal("w2", 1)
+        for o in range(PASSES):
+            deal_bytes("w2", o)
         nc.vector.tensor_copy(picked_words[1][:], x_table[1][:].bitcast(U32).indirect(offs_sb[:]))
-        deal("w1", 0)
-        deal("w1", 1)
+        for o in range(PASSES):
+            deal_bytes("w1", o)
+            deal_words("w1", o)
 
         unit_sb = keep.tile([P, PACK], F32, name="unit_sb", tag="w1_raw_words", align_bytes=64)
         nc.sync.dma_start(unit_sb[:], unit.rearrange("(p t) o -> p (t o)", t=PACK))
         w3_codes = keep.tile([P, 2 * N], U8, name="w3_codes", tag="w2_raw_words", align_bytes=64)
         nc.sync.dma_start(w3_codes[:].bitcast(I32), w3_words[0].bitcast(I32))
         w3_bytes = raw_bytes["w2"][:, 0:1, 0:N]
-        load_scale_rows(nc.sync, w3_bytes, w3_scales)
+        load_scale_rows(nc.sync, w3_bytes, w3_scales, range(QUADS))
 
         bank = {}
-        order = [("w2", t) for t in range(PACK)] + [("w1", t) for t in reversed(range(PACK))]
+        order = [("w2", t) for t in range(PACK)] + [("w1", t) for t in range(PACK)]
         for name, t in order:
             bank[name, t] = psum.tile([P, S], F32, name="bank_%s_%d" % (name, t))
 
@@ -115,48 +128,62 @@ def tile_picked_yadsiso_flux_p_kernel(
                 stop=(o == PASSES - 1),
             )
 
-        for name in ("w2", "w1"):
+        for o in range(PASSES):
+            for t in range(PACK):
+                product("w2", t, o)
+        for t in range(PACK):
             for o in range(PASSES):
-                for nm, t in order:
-                    if nm == name:
-                        product(name, t, o)
+                product("w1", t, o)
 
         side = {"w2": 0, "w1": 1}
-        exps = [work.tile([P, 2, S], F32, name="exps%d" % t, tag="chain%d" % t) for t in range(PACK)]
+        exps = work.tile([P, PACK, 2, S], F32, name="exps")
         for name, t in order:
-            nc.scalar.activation(exps[t][:, side[name], :], bank[name, t][:], ACT.Exp)
-            nc.vector.tensor_scalar(exps[t][:, side[name], :], exps[t][:, side[name], :], EXP_CAP, None, ALU.min)
+            raw_exp = work.tile([P, S], F32, name="raw_exp_%s_%d" % (name, t))
+            nc.scalar.activation(raw_exp[:], bank[name, t][:], ACT.Exp)
+            nc.vector.tensor_scalar(exps[:, t, side[name], :], raw_exp[:], EXP_CAP, None, ALU.min)
 
+        logs = work.tile([P, PACK, 2, S], F32, name="logs", tag="raw_exp_%s_%d" % order[-1])
         aff = work.tile([P, PACK, S], F32, name="aff")
         press = work.tile([P, PACK, S], F32, name="press")
-        prod = work.tile([P, PACK, S], F32, name="prod")
+        prod = [work.tile([P, S], F32, name="prod%d" % t) for t in range(PACK)]
         for t in range(PACK):
-            logs = work.tile([P, 2, S], F32, name="logs%d" % t, tag="chain%d" % (t - 1) if t else "logs")
-            nc.scalar.activation(logs[:], exps[t][:], ACT.Ln, bias=1.0)
-            nc.vector.tensor_tensor(aff[:, t, :], logs[:, 0, :], bank["w2", t][:], ALU.max)
-            nc.vector.tensor_tensor(press[:, t, :], logs[:, 1, :], bank["w1", t][:], ALU.max)
-            nc.vector.scalar_tensor_tensor(prod[:, t, :], aff[:, t, :], 0.2, press[:, t, :], ALU.add, ALU.mult)
+            if t == 0:
+                nc.scalar.activation(logs[:, t, 0, :], exps[:, t, 0, :], ACT.Ln, bias=1.0)
+                nc.scalar.activation(logs[:, t, 1, :], exps[:, t, 1, :], ACT.Ln, bias=1.0)
+            else:
+                nc.scalar.activation(logs[:, t, :, :], exps[:, t, :, :], ACT.Ln, bias=1.0)
+        for t in range(PACK):
+            nc.vector.tensor_tensor(aff[:, t, :], logs[:, t, 0, :], bank["w2", t][:], ALU.max)
+            nc.vector.tensor_tensor(press[:, t, :], logs[:, t, 1, :], bank["w1", t][:], ALU.max)
+            nc.vector.scalar_tensor_tensor(prod[t][:], aff[:, t, :], 0.2, press[:, t, :], ALU.add, ALU.mult)
 
         halves = [(h, slice(h * HALF, (h + 1) * HALF), slice(h * HALF // 16, (h + 1) * HALF // 16)) for h in range(HALVES)]
         VS = S // 2
         cross = work.tile([P, PACK, S], F32, name="cross")
-        cross_press = work.tile([P, PACK, S], F32, name="cross_press")
-
         all_dens = []
 
         def by_pair(ap):
             return ap.rearrange("p (v d) -> p v d", d=2)
 
+        def members(ap):
+            return ap.rearrange("p t (v d) -> p t v d", d=2)
+
+        kp = [work.tile([P, S], F32, name="kp%d" % t) for t in range(PACK)]
+
+        def root(t):
+            nc.scalar.activation(kp[t][:], prod[t][:], ACT.Sqrt, bias=0.02)
+
+        root(0)
         for t in range(PACK):
-            kp = work.tile([P, S], F32, name="kp%d" % t)
-            nc.scalar.activation(kp[:], prod[:, t, :], ACT.Sqrt, bias=0.02)
+            if t + 1 < PACK:
+                root(t + 1)
             rival = work.tile([P, S], F32, name="rival%d" % t)
             for h, cols, entries in halves:
-                nc.scalar.activation(rival[:, cols], kp[:].indirect(riv_sb[:, entries]), ACT.Copy)
+                nc.scalar.activation(rival[:, cols], kp[t][:].indirect(riv_sb[:, entries]), ACT.Copy)
             den = work.tile([P, S], F32, name="den%d" % t)
-            nc.vector.scalar_tensor_tensor(den[:], rival[:], 1.0, kp[:], ALU.add, ALU.add)
+            nc.vector.scalar_tensor_tensor(den[:], rival[:], 1.0, kp[t][:], ALU.add, ALU.add)
             dens = work.tile([P, 2, VS], F32, name="dens%d" % t, tag="dens%d" % t)
-            nc.vector.tensor_tensor(by_pair(cross[:, t, :]), by_pair(kp[:]), by_pair(den[:])[:, :, ::-1], ALU.mult)
+            nc.vector.tensor_tensor(by_pair(cross[:, t, :]), by_pair(kp[t][:]), by_pair(den[:])[:, :, ::-1], ALU.mult)
             nc.vector.scalar_tensor_tensor(
                 dens[:, 0, :], by_pair(den[:])[:, :, 0], 2.0, by_pair(den[:])[:, :, 1], ALU.mult, ALU.mult
             )
@@ -164,45 +191,62 @@ def tile_picked_yadsiso_flux_p_kernel(
             nc.vector.tensor_tensor(pair_sum[:], by_pair(cross[:, t, :])[:, :, 0], by_pair(cross[:, t, :])[:, :, 1], ALU.add)
             nc.vector.scalar_tensor_tensor(dens[:, 1, :], dens[:, 0, :], 0.1, pair_sum[:], ALU.mult, ALU.add)
             all_dens.append(dens)
-        log_den = work.tile([P, PACK, S], F32, name="log_den", tag="prod")
+        log_den = work.tile([P, PACK, 2, VS], F32, name="log_den", tag="prod%d" % (PACK - 1))
         for t in range(PACK):
-            nc.scalar.activation(log_den[:, t, :], all_dens[t][:].rearrange("p a v -> p (a v)"), ACT.Ln)
+            nc.scalar.activation(log_den[:, t, :, :], all_dens[t][:], ACT.Ln)
+        cross_press = work.tile([P, PACK, S], F32, name="cross_press", tag="pair_sum%d" % (PACK - 1))
         for t in range(PACK):
-            nc.vector.tensor_tensor(cross_press[:, t, :], cross[:, t, :], press[:, t, :], ALU.mult)
+            nc.vector.scalar_tensor_tensor(
+                cross_press[:, t, :], cross[:, t, :], unit_sb[:, t : t + 1], press[:, t, :], ALU.mult, ALU.mult
+            )
 
-        inv_den = work.tile([P, PACK, S], F32, name="inv_den", tag="dens%d" % (PACK - 1))
+        inv_pair = work.tile([P, PACK, VS], F32, name="inv_pair", tag="dens%d" % (PACK - 1))
+        inv_mix = work.tile([P, PACK, VS], F32, name="inv_mix", tag="exps")
+        for t in range(0, PACK, 2):
+            nc.scalar.activation(inv_pair[:, t : t + 2, :], log_den[:, t : t + 2, 0, :], ACT.Exp, scale=-1.0)
+        nc.scalar.activation(inv_mix[:], log_den[:, :, 1, :], ACT.Exp, scale=-1.0)
         flux = work.tile([P, PACK, S], F32, name="flux")
         loading = []
         for t in range(PACK):
-            nc.scalar.activation(inv_den[:, t, :], log_den[:, t, :], ACT.Exp, scale=-1.0)
             load_t = work.tile([P, S], F32, name="load%d" % t)
             nc.vector.scalar_tensor_tensor(
                 by_pair(load_t[:]), by_pair(cross[:, t, :]), unit_sb[:, t : t + 1],
-                inv_den[:, t, 0:VS].unsqueeze(2).to_broadcast([P, VS, 2]), ALU.mult, ALU.mult,
+                inv_pair[:, t, :].unsqueeze(2).to_broadcast([P, VS, 2]), ALU.mult, ALU.mult,
             )
             loading.append(load_t)
-            nc.vector.scalar_tensor_tensor(
-                by_pair(flux[:, t, :]), by_pair(cross_press[:, t, :]), unit_sb[:, t : t + 1],
-                inv_den[:, t, VS:S].unsqueeze(2).to_broadcast([P, VS, 2]), ALU.mult, ALU.mult,
-            )
 
-        for h, cols, entries in halves:
-            rival_load = work.tile([P, PACK, HALF], F32, name="rival_load%d" % h)
+        rival_loads = []
+        for h, (start, width) in enumerate(CHUNKS):
+            entries = slice(start // 16, (start + width) // 16)
+            rival_load = work.tile([P, PACK, width], F32, name="rival_load%d" % h, tag=HOLD[h])
             for t in range(PACK):
                 nc.scalar.activation(rival_load[:, t, :], loading[t][:].indirect(riv_sb[:, entries]), ACT.Copy)
-            woven = work.tile([P, HALF, PACK], BF16, name="woven%d" % h, align_bytes=64)
+            rival_loads.append(rival_load)
+        for h, (start, width) in enumerate(CHUNKS):
+            cols = slice(start, start + width)
+            nc.vector.tensor_tensor(
+                members(flux[:, :, cols]),
+                members(cross_press[:, :, cols]),
+                inv_mix[:, :, start // 2 : (start + width) // 2].unsqueeze(3).to_broadcast([P, PACK, width // 2, 2]),
+                ALU.mult,
+            )
+
+        for h, (start, width) in enumerate(CHUNKS):
+            cols = slice(start, start + width)
+            rival_load = rival_loads[h]
+            woven = work.tile([P, width, PACK], BF16, name="woven%d" % h, align_bytes=64)
             nc.vector.tensor_tensor(
                 woven[:].rearrange("p (c i) t -> p c t i", i=4),
                 flux[:, :, cols].rearrange("p t (c i) -> p c t i", i=4),
                 rival_load[:].rearrange("p t (c i) -> p c t i", i=4),
                 ALU.subtract,
             )
-            hid_codes = work.tile([P, HALF], U32, name="hid_codes%d" % h, align_bytes=64)
-            hid_bytes = work.tile([P, HALF], U8, name="hid_bytes%d" % h, align_bytes=64)
+            hid_codes = work.tile([P, width], U32, name="hid_codes%d" % h, align_bytes=64)
+            hid_bytes = work.tile([P, width], U8, name="hid_bytes%d" % h, align_bytes=64)
             nc.vector.quantize_mx(
                 out=hid_codes[:].bitcast(FP8X4), scales=hid_bytes[:], in_=woven[:].rearrange("p c t -> p (c t)")
             )
-            beds = psum.tile([P, N // P, HALF], F32, name="beds%d" % h, tag="bank_w2_%d" % h)
+            beds = psum.tile([P, N // P, width], F32, name="beds%d" % h, tag="bank_w2_%d" % h)
             for c in range(N // P):
                 nc.tensor.matmul_mx(
                     out=beds[:, c, :],
@@ -213,6 +257,9 @@ def tile_picked_yadsiso_flux_p_kernel(
                     start=True,
                     stop=True,
                 )
-            result = work.tile([P, N // P, HALF], F32, name="result%d" % h)
-            nc.scalar.copy(result[:], beds[:])
+            result = work.tile([P, N // P, width], F32, name="result%d" % h)
+            if h == len(CHUNKS) - 1:
+                nc.vector.tensor_copy(result[:], beds[:])
+            else:
+                nc.scalar.copy(result[:], beds[:])
             nc.sync.dma_start(out[:, cols].rearrange("(c p) j -> p c j", p=P), result[:])

@@ -1,3 +1,4 @@
+import math
 from contextlib import ExitStack
 
 import concourse.mybir as mybir
@@ -24,6 +25,7 @@ HALVES = 2
 HALF = S // HALVES
 CHUNKS = [(0, 256), (256, 128), (384, 128)]
 HOLD = ["rival_load0", "dens3", "cross"]
+SHIFT = math.exp(0.2)
 EXP_CAP = 2.0 ** 56
 
 
@@ -147,15 +149,12 @@ def tile_picked_yadsiso_flux_p_kernel(
         press = work.tile([P, PACK, S], F32, name="press")
         prod = [work.tile([P, S], F32, name="prod%d" % t) for t in range(PACK)]
         for t in range(PACK):
-            if t == 0:
-                nc.scalar.activation(logs[:, t, 0, :], exps[:, t, 0, :], ACT.Ln, bias=1.0)
-                nc.scalar.activation(logs[:, t, 1, :], exps[:, t, 1, :], ACT.Ln, bias=1.0)
-            else:
-                nc.scalar.activation(logs[:, t, :, :], exps[:, t, :, :], ACT.Ln, bias=1.0)
+            nc.scalar.activation(logs[:, t, 0, :], exps[:, t, 0, :], ACT.Ln, bias=SHIFT, scale=SHIFT)
+            nc.scalar.activation(logs[:, t, 1, :], exps[:, t, 1, :], ACT.Ln, bias=1.0)
         for t in range(PACK):
-            nc.vector.tensor_tensor(aff[:, t, :], logs[:, t, 0, :], bank["w2", t][:], ALU.max)
+            nc.vector.scalar_tensor_tensor(aff[:, t, :], bank["w2", t][:], 0.2, logs[:, t, 0, :], ALU.add, ALU.max)
             nc.vector.tensor_tensor(press[:, t, :], logs[:, t, 1, :], bank["w1", t][:], ALU.max)
-            nc.vector.scalar_tensor_tensor(prod[t][:], aff[:, t, :], 0.2, press[:, t, :], ALU.add, ALU.mult)
+            nc.gpsimd.tensor_tensor(prod[t][:], aff[:, t, :], press[:, t, :], ALU.mult)
 
         halves = [(h, slice(h * HALF, (h + 1) * HALF), slice(h * HALF // 16, (h + 1) * HALF // 16)) for h in range(HALVES)]
         VS = S // 2
@@ -179,7 +178,10 @@ def tile_picked_yadsiso_flux_p_kernel(
                 root(t + 1)
             rival = work.tile([P, S], F32, name="rival%d" % t)
             for h, cols, entries in halves:
-                nc.scalar.activation(rival[:, cols], kp[t][:].indirect(riv_sb[:, entries]), ACT.Copy)
+                if t == 0 and h == 1:
+                    nc.vector.tensor_copy(rival[:, cols], kp[t][:].indirect(riv_sb[:, entries]))
+                else:
+                    nc.scalar.activation(rival[:, cols], kp[t][:].indirect(riv_sb[:, entries]), ACT.Copy)
             den = work.tile([P, S], F32, name="den%d" % t)
             nc.vector.scalar_tensor_tensor(den[:], rival[:], 1.0, kp[t][:], ALU.add, ALU.add)
             dens = work.tile([P, 2, VS], F32, name="dens%d" % t, tag="dens%d" % t)
@@ -192,8 +194,10 @@ def tile_picked_yadsiso_flux_p_kernel(
             nc.vector.scalar_tensor_tensor(dens[:, 1, :], dens[:, 0, :], 0.1, pair_sum[:], ALU.mult, ALU.add)
             all_dens.append(dens)
         log_den = work.tile([P, PACK, 2, VS], F32, name="log_den", tag="prod%d" % (PACK - 1))
-        for t in range(PACK):
+        for t in range(PACK - 1):
             nc.scalar.activation(log_den[:, t, :, :], all_dens[t][:], ACT.Ln)
+        for a in range(2):
+            nc.scalar.activation(log_den[:, PACK - 1, a, :], all_dens[PACK - 1][:, a, :], ACT.Ln)
         cross_press = work.tile([P, PACK, S], F32, name="cross_press", tag="pair_sum%d" % (PACK - 1))
         for t in range(PACK):
             nc.vector.scalar_tensor_tensor(
@@ -202,8 +206,8 @@ def tile_picked_yadsiso_flux_p_kernel(
 
         inv_pair = work.tile([P, PACK, VS], F32, name="inv_pair", tag="dens%d" % (PACK - 1))
         inv_mix = work.tile([P, PACK, VS], F32, name="inv_mix", tag="exps")
-        for t in range(0, PACK, 2):
-            nc.scalar.activation(inv_pair[:, t : t + 2, :], log_den[:, t : t + 2, 0, :], ACT.Exp, scale=-1.0)
+        for tiles in (slice(0, 1), slice(1, PACK)):
+            nc.scalar.activation(inv_pair[:, tiles, :], log_den[:, tiles, 0, :], ACT.Exp, scale=-1.0)
         nc.scalar.activation(inv_mix[:], log_den[:, :, 1, :], ACT.Exp, scale=-1.0)
         flux = work.tile([P, PACK, S], F32, name="flux")
         loading = []
@@ -222,14 +226,9 @@ def tile_picked_yadsiso_flux_p_kernel(
             for t in range(PACK):
                 nc.scalar.activation(rival_load[:, t, :], loading[t][:].indirect(riv_sb[:, entries]), ACT.Copy)
             rival_loads.append(rival_load)
-        for h, (start, width) in enumerate(CHUNKS):
-            cols = slice(start, start + width)
-            nc.vector.tensor_tensor(
-                members(flux[:, :, cols]),
-                members(cross_press[:, :, cols]),
-                inv_mix[:, :, start // 2 : (start + width) // 2].unsqueeze(3).to_broadcast([P, PACK, width // 2, 2]),
-                ALU.mult,
-            )
+        nc.vector.tensor_tensor(
+            members(flux[:]), members(cross_press[:]), inv_mix[:].unsqueeze(3).to_broadcast([P, PACK, VS, 2]), ALU.mult
+        )
 
         for h, (start, width) in enumerate(CHUNKS):
             cols = slice(start, start + width)

@@ -48,17 +48,15 @@ def tile_picked_yadsiso_flux_p_kernel(
 
         offs_sb = lists.tile([P, S // 16], U16, name="offs_sb")
         riv_sb = lists.tile([P, S // 16], U16, name="riv_sb")
-        x_bytes = keep.tile([P, PASSES, T], U8, name="x_bytes", align_bytes=64)
+        x_bytes = keep.tile([P, T], U8, name="x_bytes", align_bytes=64)
         x_table = [keep.tile([P, T], I32, name="x_table%d" % o, align_bytes=64) for o in range(PASSES)]
         raw_bytes = {}
         raw_words = {}
         for name in ("w2", "w1"):
-            raw_bytes[name] = keep.tile([P, PASSES, H], U8, name=name + "_raw_bytes", align_bytes=64)
             raw_words[name] = keep.tile([P, PASSES, 2 * H], U8, name=name + "_raw_words", align_bytes=64)
-        nc.vector.memset(x_bytes[:, 0, :].bitcast(I32), 0)
-        nc.gpsimd.memset(x_bytes[:, 1, :].bitcast(I32), 0)
+        raw_bytes["w2"] = keep.tile([P, PASSES, H], U8, name="w2_raw_bytes", align_bytes=64)
+        nc.vector.memset(x_bytes[:].bitcast(I32), 0)
         nc.vector.memset(raw_bytes["w2"][:].bitcast(I32), 0)
-        nc.vector.memset(raw_bytes["w1"][:].bitcast(I32), 0)
 
         def load_table(o):
             nc.sync.dma_start(x_table[o][:], x_words[o].rearrange("p n t -> p (n t)").bitcast(I32))
@@ -68,13 +66,14 @@ def tile_picked_yadsiso_flux_p_kernel(
 
         nc.sync.dma_start(offs_sb[:], offs)
         load_words("w2", w2_words)
-        load_scale_rows(nc.sync, x_bytes, x_scales, range(QUADS))
+        for q in range(QUADS):
+            nc.sync.dma_start(
+                x_bytes[32 * q : 32 * q + 8, :].bitcast(I32), x_scales[:, 4 * q : 4 * q + 4, :].bitcast(I32)
+            )
         load_table(0)
         load_scale_rows(nc.sync, raw_bytes["w2"], w2_scales, range(QUADS))
         load_table(1)
         load_words("w1", w1_words)
-        load_scale_rows(nc.sync, raw_bytes["w1"], w1_scales, range(QUADS))
-        nc.sync.dma_start(riv_sb[:], riv)
 
         picked_words = [keep.tile([P, S], U32, name="picked_words%d" % o, align_bytes=64) for o in range(PASSES)]
         picked_bytes = [keep.tile([P, S], U8, name="picked_bytes%d" % o, align_bytes=64) for o in range(PASSES)]
@@ -90,15 +89,23 @@ def tile_picked_yadsiso_flux_p_kernel(
 
         def deal_bytes(name, o):
             planes[name, o] = keep.tile([P, H], U8, name="%s_bytes%d" % (name, o), align_bytes=64)
-            nc.vector.tensor_copy(
+            (nc.gpsimd if name == "w1" else nc.vector).tensor_copy(
                 planes[name, o][:].rearrange("p (t m) -> p t m", t=PACK),
                 raw_bytes[name][:, o, :].rearrange("p (m t) -> p t m", t=PACK),
             )
 
         for o in range(PASSES):
             deal_words("w2", o)
-        for o in range(PASSES):
-            nc.vector.tensor_copy(picked_bytes[o][:], x_bytes[:, o, :].indirect(offs_sb[:]))
+        nc.vector.tensor_copy(picked_bytes[0][:], x_bytes[:].indirect(offs_sb[:]))
+        nc.gpsimd.memset(picked_bytes[1][:].bitcast(I32), 0)
+        for q in range(QUADS):
+            nc.sync.dma_start(
+                picked_bytes[1][32 * q : 32 * q + 4, :].bitcast(I32), picked_bytes[0][32 * q + 4 : 32 * q + 8, :].bitcast(I32)
+            )
+        raw_bytes["w1"] = keep.tile([P, PASSES, H], U8, name="w1_raw_bytes", tag="x_bytes", align_bytes=64)
+        nc.vector.memset(raw_bytes["w1"][:].bitcast(I32), 0)
+        load_scale_rows(nc.sync, raw_bytes["w1"], w1_scales, range(QUADS))
+        nc.sync.dma_start(riv_sb[:], riv)
         nc.vector.tensor_copy(picked_words[0][:], x_table[0][:].bitcast(U32).indirect(offs_sb[:]))
         for o in range(PASSES):
             deal_bytes("w2", o)

import math
from contextlib import ExitStack

import concourse.mybir as mybir

K, T, S, H, N = 1024, 2048, 512, 512, 256
FLOPS = 2 * (2 * K * H * S + H * N * S)

F32 = mybir.dt.float32
BF16 = mybir.dt.bfloat16
I32 = mybir.dt.int32
U32 = mybir.dt.uint32
U16 = mybir.dt.uint16
U8 = mybir.dt.uint8
FP8X4 = mybir.dt.float8_e4m3fn_x4
FP4X4 = mybir.dt.float4_e2m1fn_x4
ALU = mybir.AluOpType
ACT = mybir.ActivationFunctionType

P = 128
PACK = 4
PASSES = K // (P * PACK)
QUADS = 4
HALVES = 2
HALF = S // HALVES
CHUNKS = [(0, 256), (256, 128), (384, 128)]
HOLD = ["rival_load0", "dens3", "cross"]
SHIFT = math.exp(0.2)
EXP_CAP = 2.0 ** 56


def tile_picked_yadsiso_flux_p_kernel(
    tc, x_words, x_scales, w1_words, w1_scales, w2_words, w2_scales, unit, w3_words, w3_scales, offs, riv, out
):
    nc = tc.nc
    with ExitStack() as ctx:
        lists = ctx.enter_context(tc.tile_pool(name="lists", bufs=1))
        keep = ctx.enter_context(tc.tile_pool(name="keep", bufs=1))
        work = ctx.enter_context(tc.tile_pool(name="work", bufs=1))
        psum = ctx.enter_context(tc.psum_pool(name="psum", bufs=1))

        def load_scale_rows(queue, tile, scales, quads):
            for q in quads:
                queue.dma_start(
                    tile[32 * q : 32 * q + 4, :, :].bitcast(I32),
                    scales[:, 4 * q : 4 * q + 4, :].rearrange("o r c -> r o c").bitcast(I32),
                )

        offs_sb = lists.tile([P, S // 16], U16, name="offs_sb")
        riv_sb = lists.tile([P, S // 16], U16, name="riv_sb")
        x_bytes = keep.tile([P, T], U8, name="x_bytes", align_bytes=64)
        x_table = [keep.tile([P, T], I32, name="x_table%d" % o, align_bytes=64) for o in range(PASSES)]
        raw_bytes = {}
        raw_words = {}
        for name in ("w2", "w1"):
            raw_words[name] = keep.tile([P, PASSES, 2 * H], U8, name=name + "_raw_words", align_bytes=64)
        raw_bytes["w2"] = keep.tile([P, PASSES, H], U8, name="w2_raw_bytes", align_bytes=64)
        nc.vector.memset(x_bytes[:].bitcast(I32), 0)
        nc.vector.memset(raw_bytes["w2"][:].bitcast(I32), 0)

        def load_table(o):
            nc.sync.dma_start(x_table[o][:], x_words[o].rearrange("p n t -> p (n t)").bitcast(I32))

        def load_words(name, words):
            nc.sync.dma_start(raw_words[name][:].bitcast(I32), words.rearrange("o p c -> p o c").bitcast(I32))

        nc.sync.dma_start(offs_sb[:], offs)
        load_words("w2", w2_words)
        for q in range(QUADS):
            nc.sync.dma_start(
                x_bytes[32 * q : 32 * q + 8, :].bitcast(I32), x_scales[:, 4 * q : 4 * q + 4, :].bitcast(I32)
            )
        load_table(0)
        load_scale_rows(nc.sync, raw_bytes["w2"], w2_scales, range(QUADS))
        load_table(1)
        load_words("w1", w1_words)

        picked_words = [keep.tile([P, S], U32, name="picked_words%d" % o, align_bytes=64) for o in range(PASSES)]
        picked_bytes = [keep.tile([P, S], U8, name="picked_bytes%d" % o, align_bytes=64) for o in range(PASSES)]
        codes = {}
        planes = {}

        def deal_words(name, o):
            codes[name, o] = keep.tile([P, 2 * H], U8, name="%s_codes%d" % (name, o), align_bytes=64)
            nc.vector.tensor_copy(
                codes[name, o][:].rearrange("p (t m b) -> p t m b", t=PACK, b=2),
                raw_words[name][:, o, :].rearrange("p (m t b) -> p t m b", t=PACK, b=2),
            )

        def deal_bytes(name, o):
            planes[name, o] = keep.tile([P, H], U8, name="%s_bytes%d" % (name, o), align_bytes=64)
            (nc.gpsimd if name == "w1" else nc.vector).tensor_copy(
                planes[name, o][:].rearrange("p (t m) -> p t m", t=PACK),
                raw_bytes[name][:, o, :].rearrange("p (m t) -> p t m", t=PACK),
            )

        for o in range(PASSES):
            deal_words("w2", o)
        nc.vector.tensor_copy(picked_bytes[0][:], x_bytes[:].indirect(offs_sb[:]))
        nc.gpsimd.memset(picked_bytes[1][:].bitcast(I32), 0)
        for q in range(QUADS):
            nc.sync.dma_start(
                picked_bytes[1][32 * q : 32 * q + 4, :].bitcast(I32), picked_bytes[0][32 * q + 4 : 32 * q + 8, :].bitcast(I32)
            )
        raw_bytes["w1"] = keep.tile([P, PASSES, H], U8, name="w1_raw_bytes", tag="x_bytes", align_bytes=64)
        nc.vector.memset(raw_bytes["w1"][:].bitcast(I32), 0)
        load_scale_rows(nc.sync, raw_bytes["w1"], w1_scales, range(QUADS))
        nc.sync.dma_start(riv_sb[:], riv)
        nc.vector.tensor_copy(picked_words[0][:], x_table[0][:].bitcast(U32).indirect(offs_sb[:]))
        for o in range(PASSES):
            deal_bytes("w2", o)
        nc.vector.tensor_copy(picked_words[1][:], x_table[1][:].bitcast(U32).indirect(offs_sb[:]))
        for o in range(PASSES):
            deal_bytes("w1", o)
            deal_words("w1", o)

        unit_sb = keep.tile([P, PACK], F32, name="unit_sb", tag="w1_raw_words", align_bytes=64)
        nc.sync.dma_start(unit_sb[:], unit.rearrange("(p t) o -> p (t o)", t=PACK))
        w3_codes = keep.tile([P, 2 * N], U8, name="w3_codes", tag="w2_raw_words", align_bytes=64)
        nc.sync.dma_start(w3_codes[:].bitcast(I32), w3_words[0].bitcast(I32))
        w3_bytes = raw_bytes["w2"][:, 0:1, 0:N]
        load_scale_rows(nc.sync, w3_bytes, w3_scales, range(QUADS))

        bank = {}
        order = [("w2", t) for t in range(PACK)] + [("w1", t) for t in range(PACK)]
        for name, t in order:
            bank[name, t] = psum.tile([P, S], F32, name="bank_%s_%d" % (name, t))

        def product(name, t, o):
            nc.tensor.matmul_mx(
                out=bank[name, t][:],
                lhsT=codes[name, o][:, 2 * P * t : 2 * P * (t + 1)].bitcast(FP4X4),
                lhsT_scale=planes[name, o][:, P * t : P * (t + 1)],
                rhs=picked_words[o][:].bitcast(FP8X4),
                rhs_scale=picked_bytes[o][:],
                start=(o == 0),
                stop=(o == PASSES - 1),
            )

        for o in range(PASSES):
            for t in range(PACK):
                product("w2", t, o)
        for t in range(PACK):
            for o in range(PASSES):
                product("w1", t, o)

        side = {"w2": 0, "w1": 1}
        exps = work.tile([P, PACK, 2, S], F32, name="exps")
        for name, t in order:
            raw_exp = work.tile([P, S], F32, name="raw_exp_%s_%d" % (name, t))
            nc.scalar.activation(raw_exp[:], bank[name, t][:], ACT.Exp)
            nc.vector.tensor_scalar(exps[:, t, side[name], :], raw_exp[:], EXP_CAP, None, ALU.min)

        logs = work.tile([P, PACK, 2, S], F32, name="logs", tag="raw_exp_%s_%d" % order[-1])
        aff = work.tile([P, PACK, S], F32, name="aff")
        press = work.tile([P, PACK, S], F32, name="press")
        prod = [work.tile([P, S], F32, name="prod%d" % t) for t in range(PACK)]
        for t in range(PACK):
            nc.scalar.activation(logs[:, t, 0, :], exps[:, t, 0, :], ACT.Ln, bias=SHIFT, scale=SHIFT)
            nc.scalar.activation(logs[:, t, 1, :], exps[:, t, 1, :], ACT.Ln, bias=1.0)
        for t in range(PACK):
            nc.vector.scalar_tensor_tensor(aff[:, t, :], bank["w2", t][:], 0.2, logs[:, t, 0, :], ALU.add, ALU.max)
            nc.vector.tensor_tensor(press[:, t, :], logs[:, t, 1, :], bank["w1", t][:], ALU.max)
            nc.gpsimd.tensor_tensor(prod[t][:], aff[:, t, :], press[:, t, :], ALU.mult)

        halves = [(h, slice(h * HALF, (h + 1) * HALF), slice(h * HALF // 16, (h + 1) * HALF // 16)) for h in range(HALVES)]
        VS = S // 2
        cross = work.tile([P, PACK, S], F32, name="cross")
        all_dens = []

        def by_pair(ap):
            return ap.rearrange("p (v d) -> p v d", d=2)

        def members(ap):
            return ap.rearrange("p t (v d) -> p t v d", d=2)

        kp = [work.tile([P, S], F32, name="kp%d" % t) for t in range(PACK)]

        def root(t):
            nc.scalar.activation(kp[t][:], prod[t][:], ACT.Sqrt, bias=0.02)

        root(0)
        for t in range(PACK):
            if t + 1 < PACK:
                root(t + 1)
            rival = work.tile([P, S], F32, name="rival%d" % t)
            for h, cols, entries in halves:
                if t == 0 and h == 1:
                    nc.vector.tensor_copy(rival[:, cols], kp[t][:].indirect(riv_sb[:, entries]))
                else:
                    nc.scalar.activation(rival[:, cols], kp[t][:].indirect(riv_sb[:, entries]), ACT.Copy)
            den = work.tile([P, S], F32, name="den%d" % t)
            nc.vector.scalar_tensor_tensor(den[:], rival[:], 1.0, kp[t][:], ALU.add, ALU.add)
            dens = work.tile([P, 2, VS], F32, name="dens%d" % t, tag="dens%d" % t)
            nc.vector.tensor_tensor(by_pair(cross[:, t, :]), by_pair(kp[t][:]), by_pair(den[:])[:, :, ::-1], ALU.mult)
            nc.vector.scalar_tensor_tensor(
                dens[:, 0, :], by_pair(den[:])[:, :, 0], 2.0, by_pair(den[:])[:, :, 1], ALU.mult, ALU.mult
            )
            pair_sum = work.tile([P, VS], F32, name="pair_sum%d" % t)
            nc.vector.tensor_tensor(pair_sum[:], by_pair(cross[:, t, :])[:, :, 0], by_pair(cross[:, t, :])[:, :, 1], ALU.add)
            nc.vector.scalar_tensor_tensor(dens[:, 1, :], dens[:, 0, :], 0.1, pair_sum[:], ALU.mult, ALU.add)
            all_dens.append(dens)
        log_den = work.tile([P, PACK, 2, VS], F32, name="log_den", tag="prod%d" % (PACK - 1))
        for t in range(PACK - 1):
            nc.scalar.activation(log_den[:, t, :, :], all_dens[t][:], ACT.Ln)
        for a in range(2):
            nc.scalar.activation(log_den[:, PACK - 1, a, :], all_dens[PACK - 1][:, a, :], ACT.Ln)
        cross_press = work.tile([P, PACK, S], F32, name="cross_press", tag="pair_sum%d" % (PACK - 1))
        for t in range(PACK):
            nc.vector.scalar_tensor_tensor(
                cross_press[:, t, :], cross[:, t, :], unit_sb[:, t : t + 1], press[:, t, :], ALU.mult, ALU.mult
            )

        inv_pair = work.tile([P, PACK, VS], F32, name="inv_pair", tag="dens%d" % (PACK - 1))
        inv_mix = work.tile([P, PACK, VS], F32, name="inv_mix", tag="exps")
        for tiles in (slice(0, 1), slice(1, PACK)):
            nc.scalar.activation(inv_pair[:, tiles, :], log_den[:, tiles, 0, :], ACT.Exp, scale=-1.0)
        nc.scalar.activation(inv_mix[:], log_den[:, :, 1, :], ACT.Exp, scale=-1.0)
        flux = work.tile([P, PACK, S], F32, name="flux")
        loading = []
        for t in range(PACK):
            load_t = work.tile([P, S], F32, name="load%d" % t)
            nc.vector.scalar_tensor_tensor(
                by_pair(load_t[:]), by_pair(cross[:, t, :]), unit_sb[:, t : t + 1],
                inv_pair[:, t, :].unsqueeze(2).to_broadcast([P, VS, 2]), ALU.mult, ALU.mult,
            )
            loading.append(load_t)

        rival_loads = []
        for h, (start, width) in enumerate(CHUNKS):
            entries = slice(start // 16, (start + width) // 16)
            rival_load = work.tile([P, PACK, width], F32, name="rival_load%d" % h, tag=HOLD[h])
            for t in range(PACK):
                nc.scalar.activation(rival_load[:, t, :], loading[t][:].indirect(riv_sb[:, entries]), ACT.Copy)
            rival_loads.append(rival_load)
        nc.vector.tensor_tensor(
            members(flux[:]), members(cross_press[:]), inv_mix[:].unsqueeze(3).to_broadcast([P, PACK, VS, 2]), ALU.mult
        )

        for h, (start, width) in enumerate(CHUNKS):
            cols = slice(start, start + width)
            rival_load = rival_loads[h]
            woven = work.tile([P, width, PACK], BF16, name="woven%d" % h, align_bytes=64)
            nc.vector.tensor_tensor(
                woven[:].rearrange("p (c i) t -> p c t i", i=4),
                flux[:, :, cols].rearrange("p t (c i) -> p c t i", i=4),
                rival_load[:].rearrange("p t (c i) -> p c t i", i=4),
                ALU.subtract,
            )
            hid_codes = work.tile([P, width], U32, name="hid_codes%d" % h, align_bytes=64)
            hid_bytes = work.tile([P, width], U8, name="hid_bytes%d" % h, align_bytes=64)
            nc.vector.quantize_mx(
                out=hid_codes[:].bitcast(FP8X4), scales=hid_bytes[:], in_=woven[:].rearrange("p c t -> p (c t)")
            )
            beds = psum.tile([P, N // P, width], F32, name="beds%d" % h, tag="bank_w2_%d" % h)
            for c in range(N // P):
                nc.tensor.matmul_mx(
                    out=beds[:, c, :],
                    lhsT=w3_codes[:, 2 * P * c : 2 * P * (c + 1)].bitcast(FP4X4),
                    lhsT_scale=w3_bytes[:, 0, P * c : P * (c + 1)],
                    rhs=hid_codes[:].bitcast(FP8X4),
                    rhs_scale=hid_bytes[:],
                    start=True,
                    stop=True,
                )
            result = work.tile([P, N // P, width], F32, name="result%d" % h)
            if h == len(CHUNKS) - 1:
                nc.vector.tensor_copy(result[:], beds[:])
            else:
                nc.scalar.copy(result[:], beds[:])
            nc.sync.dma_start(out[:, cols].rearrange("(c p) j -> p c j", p=P), result[:])
